import numpy as np, ml_dtypes
CORES = [83,219,339,475,86,222,342,478]
N = 8
F = 32
def setup_inputs(rng):
    return {"a": rng.standard_normal((N, 128, 128), dtype=np.float32).astype(ml_dtypes.bfloat16), "w": rng.standard_normal((N, 128, N * F), dtype=np.float32).astype(ml_dtypes.bfloat16)}
def reference(a, w):
    tot = np.zeros((128, N * F))
    for j in range(N):
        tot += a[j].astype(np.float64).T @ w[j].astype(np.float64)
    return {"y": np.stack([tot[:, F * r:F * r + F] for r in range(N)]).astype(ml_dtypes.bfloat16 if a.dtype != np.float64 else np.float64)}

@@ -1,0 +1,97 @@
+from concourse.bass import DstId, RemoteDMATransfer
+from concourse.mybir import AluOpType
+
+F = 32
+
+SCRATCH = {
+    "asb": ("sbuf", [128, 128], "bfloat16"),
+    "wsb": ("sbuf", [128, 256], "bfloat16"),
+    "pb": ("sbuf", [128, 224], "bfloat16"),
+    "xl": ("sbuf", [128, 64], "bfloat16"),
+    "fl": ("sbuf", [128, 160], "bfloat16"),
+    "acc": ("sbuf", [128, 128], "float32"),
+    "ysb": ("sbuf", [128, 32], "bfloat16"),
+    "ps1": ("psum", [128, 512], "float32"),
+    "ps2": ("psum", [128, 512], "float32"),
+    "ps3": ("psum", [128, 512], "float32"),
+}
+SEMAPHORES = ["ld", "mm1", "mm2", "mm3", "ev1", "ev2", "xch", "pk", "n1", "n2", "d0", "d1", "vs", "snt", "st"]
+
+
+def _b(i, n=1):
+    return slice(F * i, F * (i + n))
+
+
+def rank_program(g, core, T, topo):
+    S = T.sem
+
+    def xfer(dst, out_ap, in_ap, mask, sem):
+        rid, pid = topo.addr(dst, core)
+        return RemoteDMATransfer(dst_ids=[DstId(rid=rid, pnc=pid)], dma_engine_mask=mask, remote_sem=sem,
+                                 src=in_ap, dst=out_ap)
+
+    rank = T.rank_of(core)
+    if rank is None:
+        src = T.rank_of(core ^ 128)
+        if src is None:
+            return
+        x, s = src % 4, src // 4
+        g.wait_ge(S.xch, 8)
+        g.remote_dma_fused([xfer(T.cores[(x + 2) % 4 + 4 * t], T.fl[:, _b(3 + s)], T.xl[:, _b(t)], 0x0F << (4 * t),
+                                 S["d%d" % s]) for t in (0, 1)], local_sem=S.snt)
+        g.wait_ge(S.snt, 8)
+        return
+
+    x, s = rank % 4, rank // 4
+
+    def R(dx, t):
+        return (x + dx) % 4 + 4 * t
+
+    peer = T.cores[R(0, 1 - s)]
+    order = [R(2, 0), R(2, 1), R(1, 1 - s), R(-1, 1 - s), R(1, s), R(-1, s), R(0, 1 - s), rank]
+
+    g.sync.dma_start(T.asb[:], T.a[:]).then_inc(S.ld, 16)
+    g.scalar.dma_start(T.wsb[:], T.w[:]).then_inc(S.ld, 16)
+
+    te = g.tensor
+    te.wait_ge(S.ld, 32)
+    for i, d in enumerate(order):
+        if i < 4:
+            ps, col, sem = T.ps1, i, S.mm1
+        elif i < 7:
+            ps, col, sem = T.ps2, i - 4, S.mm2
+        else:
+            ps, col, sem = T.ps3, 0, S.mm3
+        te.matmul(ps[:, _b(col)], T.asb[:], T.wsb[:, _b(d)], True, True).then_inc(sem, 1)
+
+    v = g.vector
+    v.wait_ge(S.mm1, 4)
+    v.tensor_copy(T.pb[:, 0:128], T.ps1[:, 0:128]).then_inc(S.ev1, 1)
+    v.wait_ge(S.mm2, 3)
+    v.tensor_copy(T.pb[:, _b(6)], T.ps2[:, _b(2)]).then_inc(S.ev2, 1)
+    v.wait_ge(S.xch, 8)
+    v.tensor_tensor(T.pb[:, _b(4, 2)], T.ps2[:, _b(0, 2)], T.xl[:, 0:64], AluOpType.add).then_inc(S.ev2, 1)
+
+    g.wait_ge(S.ev1, 1)
+    g.remote_dma_fused([xfer(core ^ 128, T.xl[:, 0:64], T.pb[:, _b(0, 2)], 0x00FF, S.xch),
+                        xfer(peer, T.xl[:, 0:64], T.pb[:, _b(2, 2)], 0xFF00, S.xch)], local_sem=S.snt)
+    g.wait_ge(S.ev2, 2)
+    g.remote_dma_fused([xfer(T.cores[R(1, s)], T.fl[:, _b(1)], T.pb[:, _b(4)], 0x000F, S.n1),
+                        xfer(T.cores[R(-1, s)], T.fl[:, _b(2)], T.pb[:, _b(5)], 0x00F0, S.n2),
+                        xfer(peer, T.fl[:, _b(0)], T.pb[:, _b(6)], 0xFF00, S.pk)], local_sem=S.snt)
+
+    near = [(1, S.n1), (2, S.n2)] if x % 2 else [(2, S.n2), (1, S.n1)]
+    late = near + [(3, S.d0), (4, S.d1)]
+    v.wait_ge(S.mm3, 1)
+    v.wait_ge(S.pk, 8)
+    v.tensor_tensor(T.acc[:, _b(0)], T.ps3[:, _b(0)], T.fl[:, _b(0)], AluOpType.add).then_inc(S.vs, 1)
+    for k, (slot, sem) in enumerate(late):
+        v.wait_ge(S.vs, k + 1)
+        v.wait_ge(sem, 4)
+        out = T.ysb[:] if k == len(late) - 1 else T.acc[:, _b(k + 1)]
+        v.tensor_tensor(out, T.acc[:, _b(k)], T.fl[:, _b(slot)], AluOpType.add).then_inc(S.vs, 1)
+
+    g.sync.wait_ge(S.vs, len(late) + 1)
+    g.sync.dma_start(T.y[:], T.ysb[:]).then_inc(S.st, 16)
+    g.sync.wait_ge(S.st, 16)
+    g.wait_ge(S.snt, 32)

@@ -8,8 +8,8 @@ SCRATCH = {
     "wsb": ("sbuf", [128, 256], "bfloat16"),
     "pb": ("sbuf", [128, 224], "bfloat16"),
     "xl": ("sbuf", [128, 64], "bfloat16"),
-    "fl": ("sbuf", [128, 160], "bfloat16"),
-    "acc": ("sbuf", [128, 128], "float32"),
+    "fl": ("sbuf", [128, 224], "bfloat16"),
+    "acc": ("sbuf", [128, 192], "float32"),
     "ysb": ("sbuf", [128, 32], "bfloat16"),
     "ps1": ("psum", [128, 512], "float32"),
     "ps2": ("psum", [128, 512], "float32"),
@@ -32,12 +32,12 @@ def rank_program(g, core, T, topo):
 
     rank = T.rank_of(core)
     if rank is None:
-        src = T.rank_of(core ^ 128)
+        src = T.rank_of((core + 2) ^ 128)
         if src is None:
             return
         x, s = src % 4, src // 4
         g.wait_ge(S.xch, 8)
-        g.remote_dma_fused([xfer(T.cores[(x + 2) % 4 + 4 * t], T.fl[:, _b(3 + s)], T.xl[:, _b(t)], 0x0F << (4 * t),
+        g.remote_dma_fused([xfer(T.cores[(x + 2) % 4 + 4 * t], T.fl[:, _b(5 + s)], T.xl[:, _b(t)], 0x0F << (4 * t),
                                  S["d%d" % s]) for t in (0, 1)], local_sem=S.snt)
         g.wait_ge(S.snt, 8)
         return
@@ -48,7 +48,8 @@ def rank_program(g, core, T, topo):
         return (x + dx) % 4 + 4 * t
 
     peer = T.cores[R(0, 1 - s)]
-    order = [R(2, 0), R(2, 1), R(1, 1 - s), R(-1, 1 - s), R(1, s), R(-1, s), R(0, 1 - s), rank]
+    relay = (core ^ 128) - 2
+    order = [R(2, 0), R(2, 1), R(1, 0), R(1, 1), R(-1, 0), R(-1, 1), R(0, 1 - s), rank]
 
     g.sync.dma_start(T.asb[:], T.a[:]).then_inc(S.ld, 16)
     g.scalar.dma_start(T.wsb[:], T.w[:]).then_inc(S.ld, 16)
@@ -56,42 +57,41 @@ def rank_program(g, core, T, topo):
     te = g.tensor
     te.wait_ge(S.ld, 32)
     for i, d in enumerate(order):
-        if i < 4:
+        if i < 2:
             ps, col, sem = T.ps1, i, S.mm1
         elif i < 7:
-            ps, col, sem = T.ps2, i - 4, S.mm2
+            ps, col, sem = T.ps2, i - 2, S.mm2
         else:
             ps, col, sem = T.ps3, 0, S.mm3
         te.matmul(ps[:, _b(col)], T.asb[:], T.wsb[:, _b(d)], True, True).then_inc(sem, 1)
 
     v = g.vector
-    v.wait_ge(S.mm1, 4)
-    v.tensor_copy(T.pb[:, 0:128], T.ps1[:, 0:128]).then_inc(S.ev1, 1)
-    v.wait_ge(S.mm2, 3)
-    v.tensor_copy(T.pb[:, _b(6)], T.ps2[:, _b(2)]).then_inc(S.ev2, 1)
-    v.wait_ge(S.xch, 8)
-    v.tensor_tensor(T.pb[:, _b(4, 2)], T.ps2[:, _b(0, 2)], T.xl[:, 0:64], AluOpType.add).then_inc(S.ev2, 1)
+    v.wait_ge(S.mm1, 2)
+    v.tensor_copy(T.pb[:, _b(0, 2)], T.ps1[:, _b(0, 2)]).then_inc(S.ev1, 1)
+    v.wait_ge(S.mm2, 5)
+    v.tensor_copy(T.pb[:, _b(2, 5)], T.ps2[:, _b(0, 5)]).then_inc(S.ev2, 1)
 
     g.wait_ge(S.ev1, 1)
-    g.remote_dma_fused([xfer(core ^ 128, T.xl[:, 0:64], T.pb[:, _b(0, 2)], 0x00FF, S.xch),
-                        xfer(peer, T.xl[:, 0:64], T.pb[:, _b(2, 2)], 0xFF00, S.xch)], local_sem=S.snt)
-    g.wait_ge(S.ev2, 2)
-    g.remote_dma_fused([xfer(T.cores[R(1, s)], T.fl[:, _b(1)], T.pb[:, _b(4)], 0x000F, S.n1),
-                        xfer(T.cores[R(-1, s)], T.fl[:, _b(2)], T.pb[:, _b(5)], 0x00F0, S.n2),
+    g.remote_dma_fused([xfer(relay, T.xl[:, 0:64], T.pb[:, _b(0, 2)], 0x00FF, S.xch)], local_sem=S.snt)
+    g.wait_ge(S.ev2, 1)
+    g.remote_dma_fused([xfer(T.cores[R(1, 0)], T.fl[:, _b(1 + s)], T.pb[:, _b(2)], 0x0003, S.n1),
+                        xfer(T.cores[R(1, 1)], T.fl[:, _b(1 + s)], T.pb[:, _b(3)], 0x000C, S.n1),
+                        xfer(T.cores[R(-1, 0)], T.fl[:, _b(3 + s)], T.pb[:, _b(4)], 0x0030, S.n2),
+                        xfer(T.cores[R(-1, 1)], T.fl[:, _b(3 + s)], T.pb[:, _b(5)], 0x00C0, S.n2),
                         xfer(peer, T.fl[:, _b(0)], T.pb[:, _b(6)], 0xFF00, S.pk)], local_sem=S.snt)
 
-    near = [(1, S.n1), (2, S.n2)] if x % 2 else [(2, S.n2), (1, S.n1)]
-    late = near + [(3, S.d0), (4, S.d1)]
+    lo, hi = [(1, S.n1, 4), (2, S.n1, 4)], [(3, S.n2, 4), (4, S.n2, 4)]
+    late = (lo + hi if x % 2 else hi + lo) + [(5, S.d0, 4), (6, S.d1, 4)]
     v.wait_ge(S.mm3, 1)
     v.wait_ge(S.pk, 8)
     v.tensor_tensor(T.acc[:, _b(0)], T.ps3[:, _b(0)], T.fl[:, _b(0)], AluOpType.add).then_inc(S.vs, 1)
-    for k, (slot, sem) in enumerate(late):
+    for k, (slot, sem, n) in enumerate(late):
         v.wait_ge(S.vs, k + 1)
-        v.wait_ge(sem, 4)
+        v.wait_ge(sem, n)
         out = T.ysb[:] if k == len(late) - 1 else T.acc[:, _b(k + 1)]
         v.tensor_tensor(out, T.acc[:, _b(k)], T.fl[:, _b(slot)], AluOpType.add).then_inc(S.vs, 1)
 
     g.sync.wait_ge(S.vs, len(late) + 1)
     g.sync.dma_start(T.y[:], T.ysb[:]).then_inc(S.st, 16)
     g.sync.wait_ge(S.st, 16)
-    g.wait_ge(S.snt, 32)
+    g.wait_ge(S.snt, 24)

@@ -14,8 +14,10 @@ SCRATCH = {
     "ps1": ("psum", [128, 512], "float32"),
     "ps2": ("psum", [128, 512], "float32"),
     "ps3": ("psum", [128, 512], "float32"),
+    "ps4": ("psum", [128, 512], "float32"),
 }
-SEMAPHORES = ["ld", "mm1", "mm2", "mm3", "ev1", "ev2", "xch", "pk", "n1", "n2", "d0", "d1", "vs", "snt", "st"]
+SEMAPHORES = ["ld", "mm1", "mm2", "mm3", "mm4", "ev1", "ev2", "ev3", "xch", "pk", "a1", "a2", "a3", "a4", "d0", "d1",
+              "vs", "snt", "st"]
 
 
 def _b(i, n=1):
@@ -37,61 +39,62 @@ def rank_program(g, core, T, topo):
             return
         x, s = src % 4, src // 4
         g.wait_ge(S.xch, 8)
-        g.remote_dma_fused([xfer(T.cores[(x + 2) % 4 + 4 * t], T.fl[:, _b(5 + s)], T.xl[:, _b(t)], 0x0F << (4 * t),
-                                 S["d%d" % s]) for t in (0, 1)], local_sem=S.snt)
-        g.wait_ge(S.snt, 8)
+        for t in (s, 1 - s):
+            g.remote_dma_fused([xfer(T.cores[(x + 2) % 4 + 4 * t], T.fl[:, _b(5 + s)], T.xl[:, _b(t)], 0x00FF,
+                                     S["d%d" % s])], local_sem=S.snt)
+        g.wait_ge(S.snt, 16)
         return
 
     x, s = rank % 4, rank // 4
+    near = -1 if x % 2 else 1
+    far = -near
 
     def R(dx, t):
         return (x + dx) % 4 + 4 * t
 
     peer = T.cores[R(0, 1 - s)]
     relay = (core ^ 128) - 2
-    order = [R(2, 0), R(2, 1), R(1, 0), R(1, 1), R(-1, 0), R(-1, 1), R(0, 1 - s), rank]
+    order = [R(2, 0), R(2, 1), R(far, s), R(far, 1 - s), R(0, 1 - s), R(near, s), R(near, 1 - s), rank]
+    place = [(T.ps1, 0, S.mm1), (T.ps1, 1, S.mm1), (T.ps2, 0, S.mm2), (T.ps2, 1, S.mm2), (T.ps2, 2, S.mm2),
+             (T.ps4, 0, S.mm4), (T.ps4, 1, S.mm4), (T.ps3, 0, S.mm3)]
 
     g.sync.dma_start(T.asb[:], T.a[:]).then_inc(S.ld, 16)
     g.scalar.dma_start(T.wsb[:], T.w[:]).then_inc(S.ld, 16)
 
     te = g.tensor
     te.wait_ge(S.ld, 32)
-    for i, d in enumerate(order):
-        if i < 2:
-            ps, col, sem = T.ps1, i, S.mm1
-        elif i < 7:
-            ps, col, sem = T.ps2, i - 2, S.mm2
-        else:
-            ps, col, sem = T.ps3, 0, S.mm3
+    for d, (ps, col, sem) in zip(order, place):
         te.matmul(ps[:, _b(col)], T.asb[:], T.wsb[:, _b(d)], True, True).then_inc(sem, 1)
 
     v = g.vector
     v.wait_ge(S.mm1, 2)
     v.tensor_copy(T.pb[:, _b(0, 2)], T.ps1[:, _b(0, 2)]).then_inc(S.ev1, 1)
-    v.wait_ge(S.mm2, 5)
-    v.tensor_copy(T.pb[:, _b(2, 5)], T.ps2[:, _b(0, 5)]).then_inc(S.ev2, 1)
+    v.wait_ge(S.mm2, 3)
+    v.tensor_copy(T.pb[:, _b(2, 3)], T.ps2[:, _b(0, 3)]).then_inc(S.ev2, 1)
+    v.wait_ge(S.mm4, 2)
+    v.tensor_copy(T.pb[:, _b(5, 2)], T.ps4[:, _b(0, 2)]).then_inc(S.ev3, 1)
 
     g.wait_ge(S.ev1, 1)
     g.remote_dma_fused([xfer(relay, T.xl[:, 0:64], T.pb[:, _b(0, 2)], 0x00FF, S.xch)], local_sem=S.snt)
     g.wait_ge(S.ev2, 1)
-    g.remote_dma_fused([xfer(T.cores[R(1, 0)], T.fl[:, _b(1 + s)], T.pb[:, _b(2)], 0x0003, S.n1),
-                        xfer(T.cores[R(1, 1)], T.fl[:, _b(1 + s)], T.pb[:, _b(3)], 0x000C, S.n1),
-                        xfer(T.cores[R(-1, 0)], T.fl[:, _b(3 + s)], T.pb[:, _b(4)], 0x0030, S.n2),
-                        xfer(T.cores[R(-1, 1)], T.fl[:, _b(3 + s)], T.pb[:, _b(5)], 0x00C0, S.n2),
-                        xfer(peer, T.fl[:, _b(0)], T.pb[:, _b(6)], 0xFF00, S.pk)], local_sem=S.snt)
+    g.remote_dma_fused([xfer(T.cores[R(far, s)], T.fl[:, _b(1)], T.pb[:, _b(2)], 0x00FF, S.a1),
+                        xfer(peer, T.fl[:, _b(0)], T.pb[:, _b(4)], 0xFF00, S.pk)], local_sem=S.snt)
+    g.remote_dma_fused([xfer(T.cores[R(far, 1 - s)], T.fl[:, _b(2)], T.pb[:, _b(3)], 0x00FF, S.a2)], local_sem=S.snt)
+    g.wait_ge(S.ev3, 1)
+    g.remote_dma_fused([xfer(T.cores[R(near, s)], T.fl[:, _b(3)], T.pb[:, _b(5)], 0x00FF, S.a3)], local_sem=S.snt)
+    g.remote_dma_fused([xfer(T.cores[R(near, 1 - s)], T.fl[:, _b(4)], T.pb[:, _b(6)], 0x00FF, S.a4)], local_sem=S.snt)
 
-    lo, hi = [(1, S.n1, 4), (2, S.n1, 4)], [(3, S.n2, 4), (4, S.n2, 4)]
-    late = (lo + hi if x % 2 else hi + lo) + [(5, S.d0, 4), (6, S.d1, 4)]
+    late = [(1, S.a1), (2, S.a2), (3, S.a3), (4, S.a4), (5 + s, S["d%d" % s]), (6 - s, S["d%d" % (1 - s)])]
     v.wait_ge(S.mm3, 1)
     v.wait_ge(S.pk, 8)
     v.tensor_tensor(T.acc[:, _b(0)], T.ps3[:, _b(0)], T.fl[:, _b(0)], AluOpType.add).then_inc(S.vs, 1)
-    for k, (slot, sem, n) in enumerate(late):
+    for k, (slot, sem) in enumerate(late):
         v.wait_ge(S.vs, k + 1)
-        v.wait_ge(sem, n)
+        v.wait_ge(sem, 8)
         out = T.ysb[:] if k == len(late) - 1 else T.acc[:, _b(k + 1)]
         v.tensor_tensor(out, T.acc[:, _b(k)], T.fl[:, _b(slot)], AluOpType.add).then_inc(S.vs, 1)
 
     g.sync.wait_ge(S.vs, len(late) + 1)
     g.sync.dma_start(T.y[:], T.ysb[:]).then_inc(S.st, 16)
     g.sync.wait_ge(S.st, 16)
-    g.wait_ge(S.snt, 24)
+    g.wait_ge(S.snt, 48)

from concourse.bass import DstId, RemoteDMATransfer
from concourse.mybir import AluOpType

F = 32

SCRATCH = {
    "asb": ("sbuf", [128, 128], "bfloat16"),
    "wsb": ("sbuf", [128, 256], "bfloat16"),
    "pb": ("sbuf", [128, 224], "bfloat16"),
    "xl": ("sbuf", [128, 64], "bfloat16"),
    "fl": ("sbuf", [128, 224], "bfloat16"),
    "acc": ("sbuf", [128, 192], "float32"),
    "ysb": ("sbuf", [128, 32], "bfloat16"),
    "ps1": ("psum", [128, 512], "float32"),
    "ps2": ("psum", [128, 512], "float32"),
    "ps3": ("psum", [128, 512], "float32"),
    "ps4": ("psum", [128, 512], "float32"),
}
SEMAPHORES = ["ld", "mm1", "mm2", "mm3", "mm4", "ev1", "ev2", "ev3", "xch", "pk", "a1", "a2", "a3", "a4", "d0", "d1",
              "vs", "snt", "st"]


def _b(i, n=1):
    return slice(F * i, F * (i + n))


def rank_program(g, core, T, topo):
    S = T.sem

    def xfer(dst, out_ap, in_ap, mask, sem):
        rid, pid = topo.addr(dst, core)
        return RemoteDMATransfer(dst_ids=[DstId(rid=rid, pnc=pid)], dma_engine_mask=mask, remote_sem=sem,
                                 src=in_ap, dst=out_ap)

    rank = T.rank_of(core)
    if rank is None:
        src = T.rank_of((core + 2) ^ 128)
        if src is None:
            return
        x, s = src % 4, src // 4
        g.wait_ge(S.xch, 8)
        for t in (s, 1 - s):
            g.remote_dma_fused([xfer(T.cores[(x + 2) % 4 + 4 * t], T.fl[:, _b(5 + s)], T.xl[:, _b(t)], 0x00FF,
                                     S["d%d" % s])], local_sem=S.snt)
        g.wait_ge(S.snt, 16)
        return

    x, s = rank % 4, rank // 4
    near = -1 if x % 2 else 1
    far = -near

    def R(dx, t):
        return (x + dx) % 4 + 4 * t

    peer = T.cores[R(0, 1 - s)]
    relay = (core ^ 128) - 2
    order = [R(2, 0), R(2, 1), R(far, s), R(far, 1 - s), R(0, 1 - s), R(near, s), R(near, 1 - s), rank]
    place = [(T.ps1, 0, S.mm1), (T.ps1, 1, S.mm1), (T.ps2, 0, S.mm2), (T.ps2, 1, S.mm2), (T.ps2, 2, S.mm2),
             (T.ps4, 0, S.mm4), (T.ps4, 1, S.mm4), (T.ps3, 0, S.mm3)]

    g.sync.dma_start(T.asb[:], T.a[:]).then_inc(S.ld, 16)
    g.scalar.dma_start(T.wsb[:], T.w[:]).then_inc(S.ld, 16)

    te = g.tensor
    te.wait_ge(S.ld, 32)
    for d, (ps, col, sem) in zip(order, place):
        te.matmul(ps[:, _b(col)], T.asb[:], T.wsb[:, _b(d)], True, True).then_inc(sem, 1)

    v = g.vector
    v.wait_ge(S.mm1, 2)
    v.tensor_copy(T.pb[:, _b(0, 2)], T.ps1[:, _b(0, 2)]).then_inc(S.ev1, 1)
    v.wait_ge(S.mm2, 3)
    v.tensor_copy(T.pb[:, _b(2, 3)], T.ps2[:, _b(0, 3)]).then_inc(S.ev2, 1)
    v.wait_ge(S.mm4, 2)
    v.tensor_copy(T.pb[:, _b(5, 2)], T.ps4[:, _b(0, 2)]).then_inc(S.ev3, 1)

    g.wait_ge(S.ev1, 1)
    g.remote_dma_fused([xfer(relay, T.xl[:, 0:64], T.pb[:, _b(0, 2)], 0x00FF, S.xch)], local_sem=S.snt)
    g.wait_ge(S.ev2, 1)
    g.remote_dma_fused([xfer(T.cores[R(far, s)], T.fl[:, _b(1)], T.pb[:, _b(2)], 0x00FF, S.a1),
                        xfer(peer, T.fl[:, _b(0)], T.pb[:, _b(4)], 0xFF00, S.pk)], local_sem=S.snt)
    g.remote_dma_fused([xfer(T.cores[R(far, 1 - s)], T.fl[:, _b(2)], T.pb[:, _b(3)], 0x00FF, S.a2)], local_sem=S.snt)
    g.wait_ge(S.ev3, 1)
    g.remote_dma_fused([xfer(T.cores[R(near, s)], T.fl[:, _b(3)], T.pb[:, _b(5)], 0x00FF, S.a3)], local_sem=S.snt)
    g.remote_dma_fused([xfer(T.cores[R(near, 1 - s)], T.fl[:, _b(4)], T.pb[:, _b(6)], 0x00FF, S.a4)], local_sem=S.snt)

    late = [(1, S.a1), (2, S.a2), (3, S.a3), (4, S.a4), (5 + s, S["d%d" % s]), (6 - s, S["d%d" % (1 - s)])]
    v.wait_ge(S.mm3, 1)
    v.wait_ge(S.pk, 8)
    v.tensor_tensor(T.acc[:, _b(0)], T.ps3[:, _b(0)], T.fl[:, _b(0)], AluOpType.add).then_inc(S.vs, 1)
    for k, (slot, sem) in enumerate(late):
        v.wait_ge(S.vs, k + 1)
        v.wait_ge(sem, 8)
        out = T.ysb[:] if k == len(late) - 1 else T.acc[:, _b(k + 1)]
        v.tensor_tensor(out, T.acc[:, _b(k)], T.fl[:, _b(slot)], AluOpType.add).then_inc(S.vs, 1)

    g.sync.wait_ge(S.vs, len(late) + 1)
    g.sync.dma_start(T.y[:], T.ysb[:]).then_inc(S.st, 16)
    g.sync.wait_ge(S.st, 16)
    g.wait_ge(S.snt, 48)
